import numpy as np
import ml_dtypes

BF16 = ml_dtypes.bfloat16


def bf(x):
    return np.asarray(x, np.float32).astype(BF16)


def f32(x):
    return np.asarray(x, np.float32)


def f64(x):
    return np.asarray(x).astype(np.float64)


def striped(idx):
    return np.tile(idx.reshape(-1, 16).T, (8, 1))


def rows(idx, k):
    return np.tile(idx, (k, 1))


def look(tab, idx):
    return np.take_along_axis(f64(tab), rows(idx, len(tab)), axis=1)


K, S, V, N = 256, 2048, 1024, 1024


def silu(v):
    return v / (1.0 + np.exp(-v))


def setup_inputs():
    return {"tab": f32(np.random.standard_normal((2, K, S))), "y": f32(np.random.standard_normal((K, V))), "offs": striped(np.random.permutation(S)[:N])}


def reference(tab, y, offs):
    idx = offs[:16].T.reshape(-1)
    x = (look(tab[0], idx) - f64(y)) * (silu(look(tab[1], idx)))
    return x

@@ -1,0 +1,48 @@
+import concourse.mybir as mybir
+
+F32 = mybir.dt.float32
+U16 = mybir.dt.uint16
+SUBTRACT = mybir.AluOpType.subtract
+MULT = mybir.AluOpType.mult
+SILU = mybir.ActivationFunctionType.Silu
+
+P = 128
+GROUP = 16
+PIECE = 512
+
+
+def tile_lookup_vg_subsilu_out_kernel(tc, tab, y, offs, out):
+    nc = tc.nc
+    rows, places = tab.shape[1], tab.shape[2]
+    entries = y.shape[1]
+    blocks = rows // P
+    pieces = entries // PIECE
+
+    with (
+        tc.tile_pool(name="held", bufs=1) as held,
+        tc.tile_pool(name="work", bufs=blocks * pieces) as work,
+    ):
+        offsets = held.tile([P, entries // GROUP], U16, name="offsets")
+        nc.sync.dma_start(offsets[:], offs)
+
+        gates, values, streams = [], [], []
+        for b in range(blocks):
+            block_rows = slice(b * P, (b + 1) * P)
+            gates.append(held.tile([P, places], F32, name=f"gates{b}"))
+            values.append(held.tile([P, places], F32, name=f"values{b}"))
+            streams.append(held.tile([P, entries], F32, name=f"stream{b}"))
+            nc.sync.dma_start(gates[b][:], tab[1, block_rows, :])
+            nc.sync.dma_start(values[b][:], tab[0, block_rows, :])
+            nc.sync.dma_start(streams[b][:], y[block_rows, :])
+
+        for b in range(blocks):
+            for q in range(pieces):
+                columns = slice(q * PIECE, (q + 1) * PIECE)
+                listed = offsets[:, q * PIECE // GROUP : (q + 1) * PIECE // GROUP]
+                gate = work.tile([P, PIECE], F32, name="gate")
+                difference = work.tile([P, PIECE], F32, name="difference")
+                product = work.tile([P, PIECE], F32, name="product")
+                nc.scalar.activation(gate[:], gates[b][:].indirect(listed), SILU)
+                nc.vector.tensor_tensor(difference[:], values[b][:].indirect(listed), streams[b][:, columns], SUBTRACT)
+                nc.vector.tensor_tensor(product[:], difference[:], gate[:], MULT)
+                nc.sync.dma_start(out[b * P : (b + 1) * P, columns], product[:])

@@ -8,41 +8,69 @@ SILU = mybir.ActivationFunctionType.Silu
 
 P = 128
 GROUP = 16
-PIECE = 512
+EARLY, LATE = 0, 1
 
 
 def tile_lookup_vg_subsilu_out_kernel(tc, tab, y, offs, out):
     nc = tc.nc
-    rows, places = tab.shape[1], tab.shape[2]
+    places = tab.shape[2]
     entries = y.shape[1]
-    blocks = rows // P
-    pieces = entries // PIECE
+    half, quarter = entries // 2, entries // 4
+    values_hbm = tab[0].rearrange("(p b) s -> b p s", p=P)
+    gates_hbm = tab[1].rearrange("(p b) s -> b p s", p=P)
+    y_hbm = y.rearrange("(p b) n -> p (b n)", p=P)
+    out_hbm = out.rearrange("(p b) n -> b p n", p=P)
 
-    with (
-        tc.tile_pool(name="held", bufs=1) as held,
-        tc.tile_pool(name="work", bufs=blocks * pieces) as work,
-    ):
+    with tc.tile_pool(name="held", bufs=1) as held:
         offsets = held.tile([P, entries // GROUP], U16, name="offsets")
+        values = [held.tile([P, places], F32, name=f"values{b}") for b in (EARLY, LATE)]
+        gates = [held.tile([P, places], F32, name=f"gates{b}") for b in (EARLY, LATE)]
+        stream = held.tile([P, 2 * entries], F32, name="stream")
+        gated = [held.tile([P, entries], F32, name=f"gated{b}") for b in (EARLY, LATE)]
+        difference = [held.tile([P, entries], F32, name=f"difference{b}") for b in (EARLY, LATE)]
+        product = [held.tile([P, entries], F32, name=f"product{b}") for b in (EARLY, LATE)]
+
+        def listed(first, count):
+            return offsets[:, first // GROUP : (first + count) // GROUP]
+
+        def load_stream(b, first, last):
+            nc.sync.dma_start(stream[:, b * entries + first : last], y_hbm[:, b * entries + first : last])
+
+        def look_up_gates(b, first):
+            nc.scalar.activation(gated[b][:, first : first + half], gates[b][:].indirect(listed(first, half)), SILU)
+
+        def look_up_values(b, first, count):
+            nc.vector.tensor_tensor(
+                difference[b][:, first : first + count],
+                values[b][:].indirect(listed(first, count)),
+                stream[:, b * entries + first : b * entries + first + count],
+                SUBTRACT,
+            )
+
+        def multiply_and_store(b, first, count):
+            columns = slice(first, first + count)
+            nc.vector.tensor_tensor(product[b][:, columns], difference[b][:, columns], gated[b][:, columns], MULT)
+            nc.sync.dma_start(out_hbm[b][:, columns], product[b][:, columns])
+
+        nc.sync.dma_start(gates[EARLY][:], gates_hbm[EARLY])
         nc.sync.dma_start(offsets[:], offs)
+        nc.sync.dma_start(values[EARLY][:], values_hbm[EARLY])
+        load_stream(EARLY, 0, entries + half)
+        nc.sync.dma_start(values[LATE][:], values_hbm[LATE])
+        nc.sync.dma_start(gates[LATE][:], gates_hbm[LATE])
+        load_stream(LATE, half, entries + half + quarter)
+        load_stream(LATE, half + quarter, 2 * entries)
 
-        gates, values, streams = [], [], []
-        for b in range(blocks):
-            block_rows = slice(b * P, (b + 1) * P)
-            gates.append(held.tile([P, places], F32, name=f"gates{b}"))
-            values.append(held.tile([P, places], F32, name=f"values{b}"))
-            streams.append(held.tile([P, entries], F32, name=f"stream{b}"))
-            nc.sync.dma_start(gates[b][:], tab[1, block_rows, :])
-            nc.sync.dma_start(values[b][:], tab[0, block_rows, :])
-            nc.sync.dma_start(streams[b][:], y[block_rows, :])
+        for first in (0, half):
+            look_up_gates(EARLY, first)
+            look_up_values(EARLY, first, half)
+        multiply_and_store(EARLY, 0, entries)
 
-        for b in range(blocks):
-            for q in range(pieces):
-                columns = slice(q * PIECE, (q + 1) * PIECE)
-                listed = offsets[:, q * PIECE // GROUP : (q + 1) * PIECE // GROUP]
-                gate = work.tile([P, PIECE], F32, name="gate")
-                difference = work.tile([P, PIECE], F32, name="difference")
-                product = work.tile([P, PIECE], F32, name="product")
-                nc.scalar.activation(gate[:], gates[b][:].indirect(listed), SILU)
-                nc.vector.tensor_tensor(difference[:], values[b][:].indirect(listed), streams[b][:, columns], SUBTRACT)
-                nc.vector.tensor_tensor(product[:], difference[:], gate[:], MULT)
-                nc.sync.dma_start(out[b * P : (b + 1) * P, columns], product[:])
+        look_up_values(LATE, 0, half)
+        for first in (0, half):
+            look_up_gates(LATE, first)
+        for first in (half, half + quarter):
+            look_up_values(LATE, first, quarter)
+        multiply_and_store(LATE, 0, half)
+        for first in (half, half + quarter):
+            multiply_and_store(LATE, first, quarter)

import concourse.mybir as mybir

F32 = mybir.dt.float32
U16 = mybir.dt.uint16
SUBTRACT = mybir.AluOpType.subtract
MULT = mybir.AluOpType.mult
SILU = mybir.ActivationFunctionType.Silu

P = 128
GROUP = 16
EARLY, LATE = 0, 1


def tile_lookup_vg_subsilu_out_kernel(tc, tab, y, offs, out):
    nc = tc.nc
    places = tab.shape[2]
    entries = y.shape[1]
    half, quarter = entries // 2, entries // 4
    values_hbm = tab[0].rearrange("(p b) s -> b p s", p=P)
    gates_hbm = tab[1].rearrange("(p b) s -> b p s", p=P)
    y_hbm = y.rearrange("(p b) n -> p (b n)", p=P)
    out_hbm = out.rearrange("(p b) n -> b p n", p=P)

    with tc.tile_pool(name="held", bufs=1) as held:
        offsets = held.tile([P, entries // GROUP], U16, name="offsets")
        values = [held.tile([P, places], F32, name=f"values{b}") for b in (EARLY, LATE)]
        gates = [held.tile([P, places], F32, name=f"gates{b}") for b in (EARLY, LATE)]
        stream = held.tile([P, 2 * entries], F32, name="stream")
        gated = [held.tile([P, entries], F32, name=f"gated{b}") for b in (EARLY, LATE)]
        difference = [held.tile([P, entries], F32, name=f"difference{b}") for b in (EARLY, LATE)]
        product = [held.tile([P, entries], F32, name=f"product{b}") for b in (EARLY, LATE)]

        def listed(first, count):
            return offsets[:, first // GROUP : (first + count) // GROUP]

        def load_stream(b, first, last):
            nc.sync.dma_start(stream[:, b * entries + first : last], y_hbm[:, b * entries + first : last])

        def look_up_gates(b, first):
            nc.scalar.activation(gated[b][:, first : first + half], gates[b][:].indirect(listed(first, half)), SILU)

        def look_up_values(b, first, count):
            nc.vector.tensor_tensor(
                difference[b][:, first : first + count],
                values[b][:].indirect(listed(first, count)),
                stream[:, b * entries + first : b * entries + first + count],
                SUBTRACT,
            )

        def multiply_and_store(b, first, count):
            columns = slice(first, first + count)
            nc.vector.tensor_tensor(product[b][:, columns], difference[b][:, columns], gated[b][:, columns], MULT)
            nc.sync.dma_start(out_hbm[b][:, columns], product[b][:, columns])

        nc.sync.dma_start(gates[EARLY][:], gates_hbm[EARLY])
        nc.sync.dma_start(offsets[:], offs)
        nc.sync.dma_start(values[EARLY][:], values_hbm[EARLY])
        load_stream(EARLY, 0, entries + half)
        nc.sync.dma_start(values[LATE][:], values_hbm[LATE])
        nc.sync.dma_start(gates[LATE][:], gates_hbm[LATE])
        load_stream(LATE, half, entries + half + quarter)
        load_stream(LATE, half + quarter, 2 * entries)

        for first in (0, half):
            look_up_gates(EARLY, first)
            look_up_values(EARLY, first, half)
        multiply_and_store(EARLY, 0, entries)

        look_up_values(LATE, 0, half)
        for first in (0, half):
            look_up_gates(LATE, first)
        for first in (half, half + quarter):
            look_up_values(LATE, first, quarter)
        multiply_and_store(LATE, 0, half)
        for first in (half, half + quarter):
            multiply_and_store(LATE, first, quarter)
